import numpy as np
import ml_dtypes


def mxq(x, axis, fmt="e4m3"):
    dtype, down = {"e4m3": (ml_dtypes.float8_e4m3fn, 7), "e5m2": (ml_dtypes.float8_e5m2, 14)}[fmt]
    v = np.moveaxis(np.asarray(x, np.float32).astype(ml_dtypes.bfloat16).astype(np.float64), axis, -1)
    blocks = v.reshape(v.shape[:-1] + (-1, 32))
    amax = np.abs(blocks).max(-1, keepdims=True)
    byte = np.maximum(np.where(amax > 0, np.frexp(amax)[1] - 1 + 127, 0) - down, 1)
    scale = np.exp2(byte - 127.0)
    codes = (blocks / scale).astype(np.float32).astype(dtype).astype(np.float64)
    return np.moveaxis((codes * scale).reshape(v.shape), -1, axis)


WIDE = False


def mx_kscale(k):
    if not WIDE:
        return np.ones(k)
    levels = np.array([10, -10, 5, -5, 0])
    if k % 512:
        return np.exp2(np.random.permutation(np.resize(levels, k // 32))).repeat(32)
    a = np.empty((k // 512, 16))
    for p in range(k // 512):
        a[p, :8] = np.random.permutation(np.resize(levels, 8))
        for g in range(8):
            far = levels[np.abs(levels - a[p, g]) >= 10]
            a[p, g + 8] = far[np.random.randint(len(far))]
    return np.exp2(a.ravel()).repeat(32)


def f64(x):
    return np.asarray(x).astype(np.float64)


def striped(idx):
    return np.tile(idx.reshape(-1, 16).T, (8, 1)).astype(np.uint16)


def unstriped(offs):
    return offs[:16].T.reshape(-1).astype(np.int64)


def pack_weight(w):
    k, n = w.shape
    w = f64(np.asarray(w, np.float32).astype(ml_dtypes.bfloat16)).reshape(k // 32, 32, n)
    amax = np.abs(w).max(1)
    byte = np.clip(np.where(amax > 0, np.frexp(amax)[1] - 1 + 127 - 7, 1), 1, 254)
    scaled = (w * np.exp2(127.0 - byte)[:, None, :]).reshape(k, n).astype(np.float32)
    words = np.ascontiguousarray(scaled.reshape(k // 512, 128, 4, n).transpose(0, 1, 3, 2)).astype(ml_dtypes.float8_e4m3fn).view(np.uint8)
    return words, np.ascontiguousarray(byte.astype(np.uint8).reshape(k // 512, 16, n))


def unpack_weight(words, scales):
    g, p, n, _ = words.shape
    vals = np.ascontiguousarray(words).view(ml_dtypes.float8_e4m3fn).astype(np.float64) * np.repeat(np.exp2(scales.astype(np.float64) - 127.0), 8, axis=1)[..., None]
    return vals.transpose(0, 1, 3, 2).reshape(g * 512, n)


K, T, S, N, D, U, V = 512, 1024, 512, 256, 4, 512, 128
P = 2 ** 7


def setup_inputs():
    n = np.random.standard_normal
    s = mx_kscale(K)[:, None]
    packed_xT = pack_weight(n((K, T)) * s)
    return {
        "x_words": packed_xT[0],
        "x_scales": packed_xT[1],
        "w1": (n((K, N)) / np.sqrt(K) / s).astype(np.float32),
        "field": (np.tile(n(U) * 0.7, (P, 1))).astype(np.float32),
        "lam": (np.random.uniform(0.5, 1.5, (N, 1))).astype(np.float32),
        "beta": (-np.random.uniform(0.1, 0.35, (N, 1))).astype(np.float32),
        "coup": (np.tile(np.random.uniform(0.3, 1.2, U), (P, 1))).astype(np.float32),
        "offs": striped(np.random.permutation(T)[:S]),
        "src": striped(np.repeat(np.random.permutation(S)[:V], D)),
        "dst": striped(np.random.randint(0, S, U)),
    }


def reference(x_words, x_scales, w1, field, lam, beta, coup, offs, src, dst):
    xq = unpack_weight(x_words, x_scales)[:, unstriped(offs)]
    y = mxq(f64(w1), 0, "e4m3").T @ xq
    dg = y[:, unstriped(dst)] - y[:, unstriped(src)] + f64(field)[:1]
    de = dg + f64(lam)
    rate = (np.exp(f64(beta) * ((de) ** 2))) * f64(coup)[:1]
    tot = rate.reshape(len(rate), -1, D).sum(axis=2)
    return rate / np.repeat(tot, D, axis=1)

@@ -1,0 +1,182 @@
+from contextlib import ExitStack
+
+import concourse.mybir as mybir
+from concourse.masks import make_identity
+
+K, T, S, N, D = 512, 1024, 512, 256, 4
+P = 128
+V = S // D
+HALF = S // 2
+VH = V // 2
+FLOPS = 2 * K * N * S
+
+F32 = mybir.dt.float32
+BF16 = mybir.dt.bfloat16
+I32 = mybir.dt.int32
+U32 = mybir.dt.uint32
+U16 = mybir.dt.uint16
+U8 = mybir.dt.uint8
+FP8X4 = mybir.dt.float8_e4m3fn_x4
+ALU = mybir.AluOpType
+ACT = mybir.ActivationFunctionType
+AX = mybir.AxisListType
+
+
+def tile_picked_yrates_prob_p_kernel(
+    tc, x_words, x_scales, w1, field, lam, beta, coup, offs, src, dst, out
+):
+    nc = tc.nc
+    tiles = N // P
+    with ExitStack() as ctx:
+        keep = ctx.enter_context(tc.tile_pool(name="keep", bufs=1))
+        psum = ctx.enter_context(tc.psum_pool(name="psum", bufs=1))
+
+        def bank(b, shape, name):
+            return psum.tile(shape, F32, name=name, tag="bank%d" % b)
+
+        offs_sb = keep.tile([P, S // 16], U16, name="offs_sb")
+        src_sb = keep.tile([P, S // 16], U16, name="src_sb")
+        dst_sb = keep.tile([P, S // 16], U16, name="dst_sb")
+        xw = keep.tile([P, T], I32, name="xw")
+        xs = keep.tile([P, T], U8, name="xs")
+        w_raw = keep.tile([P, 4, N], F32, name="w_raw")
+        field_sb = keep.tile([P, S], F32, name="field_sb")
+        coup_v = keep.tile([P, D], F32, name="coup_v", tag="w_bf0", align_bytes=64)
+        beta_sb = keep.tile([P, tiles], F32, name="beta_sb")
+        lam_sb = keep.tile([P, tiles], F32, name="lam_sb")
+
+        nc.gpsimd.memset(xs[:].bitcast(I32), 0)
+        nc.sync.dma_start(offs_sb[:], offs)
+        nc.sync.dma_start(out=w_raw[:], in_=w1.rearrange("(p j) n -> p j n", j=4))
+        nc.sync.dma_start(out=xw[:], in_=x_words[0].rearrange("p c r -> p (c r)").bitcast(I32))
+        nc.scalar.dma_start(out=coup_v[:], in_=coup[0].rearrange("(v d) -> v d", d=D))
+        for q in range(4):
+            nc.scalar.dma_start(
+                out=xs[32 * q : 32 * q + 4, :].bitcast(I32),
+                in_=x_scales[0, 4 * q : 4 * q + 4, :].bitcast(I32),
+            )
+        with nc.allow_non_contiguous_dma(reason="one value a partition"):
+            nc.gpsimd.dma_start(out=beta_sb[:], in_=beta.rearrange("(t p) o -> p (t o)", p=P))
+            nc.gpsimd.dma_start(out=lam_sb[:], in_=lam.rearrange("(t p) o -> p (t o)", p=P))
+        nc.sync.dma_start(src_sb[:], src)
+        nc.sync.dma_start(out=field_sb[:], in_=field)
+        nc.sync.dma_start(dst_sb[:], dst)
+
+        lnc = keep.tile([P, D], F32, name="lnc")
+        nc.scalar.activation(lnc[:], coup_v[:], ACT.Ln, bias=2.0**-64)
+        nbeta = keep.tile([P, tiles], F32, name="nbeta")
+        half_c = keep.tile([P, tiles], F32, name="half_c")
+        root = keep.tile([P, tiles], F32, name="root")
+        root_lam = keep.tile([P, tiles], F32, name="root_lam")
+        nc.gpsimd.memset(half_c[:], 0.5)
+        nc.gpsimd.tensor_scalar(nbeta[:], beta_sb[:], -1.0, 0.0, ALU.mult, ALU.add)
+        nc.gpsimd.tensor_tensor(root[:], nbeta[:], half_c[:], ALU.pow)
+        nc.gpsimd.tensor_tensor(root_lam[:], root[:], lam_sb[:], ALU.mult)
+        ident = keep.tile([P, P], F32, name="ident")
+        make_identity(nc, ident[:])
+
+        xg = keep.tile([P, S], U32, name="xg", align_bytes=64)
+        sg = keep.tile([P, S], U8, name="sg", align_bytes=64)
+        nc.vector.tensor_copy(sg[:], xs[:].indirect(offs_sb[:]))
+        w_codes, w_scales = [], []
+        w_bf = []
+        for t in range(tiles):
+            wb = keep.tile([P, P, 4], BF16, name="w_bf%d" % t, tag="w_bf%d" % t, align_bytes=64)
+            nc.scalar.copy(out=wb[:], in_=w_raw[:, :, t * P : (t + 1) * P].rearrange("p j m -> p m j"))
+            w_bf.append(wb)
+            w_codes.append(keep.tile([P, P], U32, name="w_codes%d" % t, align_bytes=64))
+            w_scales.append(keep.tile([P, P], U8, name="w_scales%d" % t, align_bytes=64))
+
+        def quantise(t):
+            nc.vector.quantize_mx(
+                out=w_codes[t][:].bitcast(FP8X4),
+                scales=w_scales[t][:],
+                in_=w_bf[t][:].rearrange("p m j -> p (m j)"),
+            )
+
+        def cols(h):
+            return slice(h * HALF, (h + 1) * HALF)
+
+        def lcols(h):
+            return slice(h * HALF // 16, (h + 1) * HALF // 16)
+
+        def groups(h):
+            return slice(h * VH, (h + 1) * VH)
+
+        def product(acc, t, c):
+            nc.tensor.matmul_mx(
+                out=acc,
+                lhsT=w_codes[t][:].bitcast(FP8X4),
+                lhsT_scale=w_scales[t][:],
+                rhs=xg[:, c].bitcast(FP8X4),
+                rhs_scale=sg[:, c],
+                start=True,
+                stop=True,
+            )
+
+        y = [keep.tile([P, S], F32, name="y%d" % t) for t in range(tiles)]
+        quantise(0)
+        quantise(1)
+        for h in range(2):
+            nc.vector.tensor_copy(xg[:, cols(h)], xw[:].bitcast(U32).indirect(offs_sb[:, lcols(h)]))
+        acc_a = bank(0, [P, HALF], "acc_a")
+        acc_b = bank(1, [P, HALF], "acc_b")
+        acc_1 = bank(2, [P, S], "acc_1")
+        product(acc_a[:], 0, cols(0))
+        nc.scalar.copy(out=y[0][:, cols(0)], in_=acc_a[:])
+        product(acc_b[:], 0, cols(1))
+        nc.vector.tensor_copy(out=y[0][:, cols(1)], in_=acc_b[:])
+        product(acc_1[:], 1, slice(0, S))
+        nc.scalar.copy(out=y[1][:], in_=acc_1[:])
+        warm = keep.tile([P, 1], F32, name="warm")
+        nc.scalar.activation(warm[:], y[1][:, S - 1 : S], ACT.Exp, scale=0.0)
+
+        for t in range(tiles):
+            part = keep.tile([P, S], F32, name="part%d" % t)
+            dg = keep.tile([P, S], F32, name="dg%d" % t)
+            sq = keep.tile([P, D, V], F32, name="sq%d" % t)
+            nmu = keep.tile([P, V], F32, name="nmu%d" % t)
+            sq_vd = sq[:].rearrange("p d v -> p v d")
+            for h in range(2):
+                nc.vector.tensor_tensor(
+                    part[:, cols(h)], y[t][:].indirect(src_sb[:, lcols(h)]), field_sb[:, cols(h)], ALU.subtract
+                )
+            for h in range(2):
+                nc.vector.tensor_tensor(
+                    dg[:, cols(h)], y[t][:].indirect(dst_sb[:, lcols(h)]), part[:, cols(h)], ALU.subtract
+                )
+                nc.scalar.activation(
+                    sq_vd[:, groups(h), :],
+                    dg[:, cols(h)].rearrange("p (v d) -> p v d", d=D),
+                    ACT.Square,
+                    bias=root_lam[:, t : t + 1],
+                    scale=root[:, t : t + 1],
+                )
+            for h in range(2):
+                nc.vector.tensor_reduce(nmu[:, groups(h)], sq_vd[:, groups(h), :], AX.X, ALU.min, negate=True)
+            turned = [bank(d, [P, P], "turned%d_%d" % (t, d)) for d in range(D)]
+            for d in range(D):
+                nc.tensor.matmul(turned[d][:], sq[:, d, :], ident[:], start=True, stop=False, is_transpose=True)
+            rate = keep.tile([P, D, P], F32, name="rate%d" % t)
+            back = bank(4 + 2 * t, [P, D, V], "back%d" % t)
+            tot = bank(5 + 2 * t, [P, V], "tot%d" % t)
+            for d in range(D):
+                nc.tensor.matmul(turned[d][:], nmu[:], ident[:], start=False, stop=True, is_transpose=True)
+            for d in range(D):
+                nc.scalar.activation(rate[:, d, :], turned[d][:], ACT.Exp, bias=lnc[:, d : d + 1], scale=-1.0)
+                nc.tensor.matmul(
+                    tot[:], rate[:, d, :], ident[:], start=(d == 0), stop=(d == D - 1), is_transpose=True
+                )
+                nc.tensor.transpose(back[:, d, :], rate[:, d, :], ident[:])
+            inv = keep.tile([P, V], F32, name="inv%d" % t)
+            res = keep.tile([P, S], F32, name="res%d" % t)
+            for h in range(2):
+                nc.vector.reciprocal(inv[:, groups(h)], tot[:, groups(h)])
+            for h in range(2):
+                nc.vector.tensor_tensor(
+                    res[:, cols(h)].rearrange("p (v d) -> p v d", d=D),
+                    back[:].rearrange("p d v -> p v d")[:, groups(h), :],
+                    inv[:, groups(h)].unsqueeze(2).to_broadcast([P, VH, D]),
+                    ALU.mult,
+                )
+                nc.sync.dma_start(out=out[t * P : (t + 1) * P, cols(h)], in_=res[:, cols(h)])

@@ -39,50 +39,44 @@ def tile_picked_yrates_prob_p_kernel(
         dst_sb = keep.tile([P, S // 16], U16, name="dst_sb")
         xw = keep.tile([P, T], I32, name="xw")
         xs = keep.tile([P, T], U8, name="xs")
-        w_raw = keep.tile([P, 4, N], F32, name="w_raw")
+        w_raw = [keep.tile([P, 4, P], F32, name="w_raw%d" % t, tag="w_raw%d" % t, align_bytes=64) for t in range(tiles)]
         field_sb = keep.tile([P, S], F32, name="field_sb")
         coup_v = keep.tile([P, D], F32, name="coup_v", tag="w_bf0", align_bytes=64)
         beta_sb = keep.tile([P, tiles], F32, name="beta_sb")
         lam_sb = keep.tile([P, tiles], F32, name="lam_sb")
 
         nc.gpsimd.memset(xs[:].bitcast(I32), 0)
-        nc.sync.dma_start(offs_sb[:], offs)
-        nc.sync.dma_start(out=w_raw[:], in_=w1.rearrange("(p j) n -> p j n", j=4))
         nc.sync.dma_start(out=xw[:], in_=x_words[0].rearrange("p c r -> p (c r)").bitcast(I32))
+        nc.sync.dma_start(offs_sb[:], offs)
         nc.scalar.dma_start(out=coup_v[:], in_=coup[0].rearrange("(v d) -> v d", d=D))
+        w_rows = w1.rearrange("(p j) n -> p j n", j=4)
+        nc.sync.dma_start(out=w_raw[0][:], in_=w_rows[:, :, 0:P])
         for q in range(4):
-            nc.scalar.dma_start(
+            nc.sync.dma_start(
                 out=xs[32 * q : 32 * q + 4, :].bitcast(I32),
                 in_=x_scales[0, 4 * q : 4 * q + 4, :].bitcast(I32),
             )
+        nc.sync.dma_start(out=w_raw[1][:], in_=w_rows[:, :, P : 2 * P])
         with nc.allow_non_contiguous_dma(reason="one value a partition"):
-            nc.gpsimd.dma_start(out=beta_sb[:], in_=beta.rearrange("(t p) o -> p (t o)", p=P))
-            nc.gpsimd.dma_start(out=lam_sb[:], in_=lam.rearrange("(t p) o -> p (t o)", p=P))
+            nc.sync.dma_start(out=beta_sb[:], in_=beta.rearrange("(t p) o -> p (t o)", p=P))
         nc.sync.dma_start(src_sb[:], src)
         nc.sync.dma_start(out=field_sb[:], in_=field)
         nc.sync.dma_start(dst_sb[:], dst)
+        with nc.allow_non_contiguous_dma(reason="one value a partition"):
+            nc.sync.dma_start(out=lam_sb[:], in_=lam.rearrange("(t p) o -> p (t o)", p=P))
 
         lnc = keep.tile([P, D], F32, name="lnc")
         nc.scalar.activation(lnc[:], coup_v[:], ACT.Ln, bias=2.0**-64)
-        nbeta = keep.tile([P, tiles], F32, name="nbeta")
-        half_c = keep.tile([P, tiles], F32, name="half_c")
-        root = keep.tile([P, tiles], F32, name="root")
-        root_lam = keep.tile([P, tiles], F32, name="root_lam")
-        nc.gpsimd.memset(half_c[:], 0.5)
-        nc.gpsimd.tensor_scalar(nbeta[:], beta_sb[:], -1.0, 0.0, ALU.mult, ALU.add)
-        nc.gpsimd.tensor_tensor(root[:], nbeta[:], half_c[:], ALU.pow)
-        nc.gpsimd.tensor_tensor(root_lam[:], root[:], lam_sb[:], ALU.mult)
         ident = keep.tile([P, P], F32, name="ident")
         make_identity(nc, ident[:])
 
         xg = keep.tile([P, S], U32, name="xg", align_bytes=64)
-        sg = keep.tile([P, S], U8, name="sg", align_bytes=64)
-        nc.vector.tensor_copy(sg[:], xs[:].indirect(offs_sb[:]))
+        nc.vector.tensor_copy(xg[:], xw[:].bitcast(U32).indirect(offs_sb[:]))
         w_codes, w_scales = [], []
         w_bf = []
         for t in range(tiles):
             wb = keep.tile([P, P, 4], BF16, name="w_bf%d" % t, tag="w_bf%d" % t, align_bytes=64)
-            nc.scalar.copy(out=wb[:], in_=w_raw[:, :, t * P : (t + 1) * P].rearrange("p j m -> p m j"))
+            nc.scalar.copy(out=wb[:], in_=w_raw[t][:].rearrange("p j m -> p m j"))
             w_bf.append(wb)
             w_codes.append(keep.tile([P, P], U32, name="w_codes%d" % t, align_bytes=64))
             w_scales.append(keep.tile([P, P], U8, name="w_scales%d" % t, align_bytes=64))
@@ -115,51 +109,66 @@ def tile_picked_yrates_prob_p_kernel(
             )
 
         y = [keep.tile([P, S], F32, name="y%d" % t) for t in range(tiles)]
+        early, late = slice(0, S - P), slice(S - P, S)
+
+        def entries(c):
+            return slice(c.start // 16, c.stop // 16)
+
         quantise(0)
+        sg = keep.tile([P, S], U8, name="sg", tag="w_raw0", align_bytes=64)
+        thirds = (slice(0, HALF), slice(HALF, S - P), late)
+        for c in thirds:
+            nc.vector.tensor_copy(sg[:, c], xs[:].indirect(offs_sb[:, entries(c)]))
+        lnb = keep.tile([P, tiles], F32, name="lnb")
+        nc.scalar.activation(lnb[:], beta_sb[:], ACT.Ln, bias=2.0**-64, scale=-1.0)
+        root = keep.tile([P, tiles], F32, name="root", tag="w_raw1", align_bytes=64)
+        root_lam = keep.tile([P, tiles], F32, name="root_lam")
+        nc.scalar.activation(root[:], lnb[:], ACT.Exp, scale=0.5)
+        for t in range(tiles):
+            nc.scalar.activation(root_lam[:, t : t + 1], lam_sb[:, t : t + 1], ACT.Copy, scale=root[:, t : t + 1])
+        accs = [bank(b, [P, c.stop - c.start], "acc%d" % b) for b, c in enumerate(thirds)]
+        for acc, c in zip(accs, thirds):
+            product(acc[:], 0, c)
         quantise(1)
-        for h in range(2):
-            nc.vector.tensor_copy(xg[:, cols(h)], xw[:].bitcast(U32).indirect(offs_sb[:, lcols(h)]))
-        acc_a = bank(0, [P, HALF], "acc_a")
-        acc_b = bank(1, [P, HALF], "acc_b")
-        acc_1 = bank(2, [P, S], "acc_1")
-        product(acc_a[:], 0, cols(0))
-        nc.scalar.copy(out=y[0][:, cols(0)], in_=acc_a[:])
-        product(acc_b[:], 0, cols(1))
-        nc.vector.tensor_copy(out=y[0][:, cols(1)], in_=acc_b[:])
+        for acc, c in zip(accs, thirds):
+            nc.vector.tensor_copy(out=y[0][:, c], in_=acc[:])
+        acc_1 = bank(3, [P, S], "acc_1")
         product(acc_1[:], 1, slice(0, S))
         nc.scalar.copy(out=y[1][:], in_=acc_1[:])
-        warm = keep.tile([P, 1], F32, name="warm")
-        nc.scalar.activation(warm[:], y[1][:, S - 1 : S], ACT.Exp, scale=0.0)
 
+        backs, tots = [], []
         for t in range(tiles):
-            part = keep.tile([P, S], F32, name="part%d" % t)
-            dg = keep.tile([P, S], F32, name="dg%d" % t)
-            sq = keep.tile([P, D, V], F32, name="sq%d" % t)
-            nmu = keep.tile([P, V], F32, name="nmu%d" % t)
+            part = [
+                keep.tile([P, HALF], F32, name="part%d_%d" % (t, h), tag="dg0" if (t, h) == (1, 1) else "part%d_%d" % (t, h))
+                for h in range(2)
+            ]
+            dg = keep.tile([P, S], F32, name="dg%d" % t, tag="dg%d" % t)
+            sq = keep.tile([P, D, V], F32, name="sq%d" % t, tag=("sq0", "chain")[t])
+            nmu = keep.tile([P, V], F32, name="nmu%d" % t, tag=("chain", "nmu1")[t])
             sq_vd = sq[:].rearrange("p d v -> p v d")
             for h in range(2):
                 nc.vector.tensor_tensor(
-                    part[:, cols(h)], y[t][:].indirect(src_sb[:, lcols(h)]), field_sb[:, cols(h)], ALU.subtract
+                    part[h][:], y[t][:].indirect(src_sb[:, lcols(h)]), field_sb[:, cols(h)], ALU.subtract
                 )
-            for h in range(2):
-                nc.vector.tensor_tensor(
-                    dg[:, cols(h)], y[t][:].indirect(dst_sb[:, lcols(h)]), part[:, cols(h)], ALU.subtract
-                )
+            pieces = [cols(0), cols(1)] if t == 0 else [cols(0), slice(HALF, S - P), late]
+            for c in pieces:
+                g = slice(c.start // D, c.stop // D)
+                nc.vector.tensor_tensor(dg[:, c], y[t][:].indirect(dst_sb[:, entries(c)]), part[c.start // HALF][:, c.start % HALF : c.start % HALF + c.stop - c.start], ALU.subtract)
                 nc.scalar.activation(
-                    sq_vd[:, groups(h), :],
-                    dg[:, cols(h)].rearrange("p (v d) -> p v d", d=D),
+                    sq_vd[:, g, :],
+                    dg[:, c].rearrange("p (v d) -> p v d", d=D),
                     ACT.Square,
                     bias=root_lam[:, t : t + 1],
                     scale=root[:, t : t + 1],
                 )
-            for h in range(2):
-                nc.vector.tensor_reduce(nmu[:, groups(h)], sq_vd[:, groups(h), :], AX.X, ALU.min, negate=True)
-            turned = [bank(d, [P, P], "turned%d_%d" % (t, d)) for d in range(D)]
+            for c in ([slice(0, S)] if t == 0 else [early, late]):
+                g = slice(c.start // D, c.stop // D)
+                nc.vector.tensor_reduce(nmu[:, g], sq_vd[:, g, :], AX.X, ALU.min, negate=True)
+            turned = [bank((0, 1, 2, 6 + t)[d], [P, P], "turned%d_%d" % (t, d)) for d in range(D)]
             for d in range(D):
                 nc.tensor.matmul(turned[d][:], sq[:, d, :], ident[:], start=True, stop=False, is_transpose=True)
             rate = keep.tile([P, D, P], F32, name="rate%d" % t)
-            back = bank(4 + 2 * t, [P, D, V], "back%d" % t)
-            tot = bank(5 + 2 * t, [P, V], "tot%d" % t)
+            tot = bank(4 + t, [P, V], "tot%d" % t)
             for d in range(D):
                 nc.tensor.matmul(turned[d][:], nmu[:], ident[:], start=False, stop=True, is_transpose=True)
             for d in range(D):
@@ -167,8 +176,15 @@ def tile_picked_yrates_prob_p_kernel(
                 nc.tensor.matmul(
                     tot[:], rate[:, d, :], ident[:], start=(d == 0), stop=(d == D - 1), is_transpose=True
                 )
+            back = bank(6 + t, [P, D, V], "back%d" % t)
+            for d in range(D):
                 nc.tensor.transpose(back[:, d, :], rate[:, d, :], ident[:])
-            inv = keep.tile([P, V], F32, name="inv%d" % t)
+            backs.append(back)
+            tots.append(tot)
+
+        for t in range(tiles):
+            back, tot = backs[t], tots[t]
+            inv = keep.tile([P, V], F32, name="inv%d" % t, tag=("dg1", "inv1")[t])
             res = keep.tile([P, S], F32, name="res%d" % t)
             for h in range(2):
                 nc.vector.reciprocal(inv[:, groups(h)], tot[:, groups(h)])

from contextlib import ExitStack

import concourse.mybir as mybir
from concourse.masks import make_identity

K, T, S, N, D = 512, 1024, 512, 256, 4
P = 128
V = S // D
HALF = S // 2
VH = V // 2
FLOPS = 2 * K * N * S

F32 = mybir.dt.float32
BF16 = mybir.dt.bfloat16
I32 = mybir.dt.int32
U32 = mybir.dt.uint32
U16 = mybir.dt.uint16
U8 = mybir.dt.uint8
FP8X4 = mybir.dt.float8_e4m3fn_x4
ALU = mybir.AluOpType
ACT = mybir.ActivationFunctionType
AX = mybir.AxisListType


def tile_picked_yrates_prob_p_kernel(
    tc, x_words, x_scales, w1, field, lam, beta, coup, offs, src, dst, out
):
    nc = tc.nc
    tiles = N // P
    with ExitStack() as ctx:
        keep = ctx.enter_context(tc.tile_pool(name="keep", bufs=1))
        psum = ctx.enter_context(tc.psum_pool(name="psum", bufs=1))

        def bank(b, shape, name):
            return psum.tile(shape, F32, name=name, tag="bank%d" % b)

        offs_sb = keep.tile([P, S // 16], U16, name="offs_sb")
        src_sb = keep.tile([P, S // 16], U16, name="src_sb")
        dst_sb = keep.tile([P, S // 16], U16, name="dst_sb")
        xw = keep.tile([P, T], I32, name="xw")
        xs = keep.tile([P, T], U8, name="xs")
        w_raw = [keep.tile([P, 4, P], F32, name="w_raw%d" % t, tag="w_raw%d" % t, align_bytes=64) for t in range(tiles)]
        field_sb = keep.tile([P, S], F32, name="field_sb")
        coup_v = keep.tile([P, D], F32, name="coup_v", tag="w_bf0", align_bytes=64)
        beta_sb = keep.tile([P, tiles], F32, name="beta_sb")
        lam_sb = keep.tile([P, tiles], F32, name="lam_sb")

        nc.gpsimd.memset(xs[:].bitcast(I32), 0)
        nc.sync.dma_start(out=xw[:], in_=x_words[0].rearrange("p c r -> p (c r)").bitcast(I32))
        nc.sync.dma_start(offs_sb[:], offs)
        nc.scalar.dma_start(out=coup_v[:], in_=coup[0].rearrange("(v d) -> v d", d=D))
        w_rows = w1.rearrange("(p j) n -> p j n", j=4)
        nc.sync.dma_start(out=w_raw[0][:], in_=w_rows[:, :, 0:P])
        for q in range(4):
            nc.sync.dma_start(
                out=xs[32 * q : 32 * q + 4, :].bitcast(I32),
                in_=x_scales[0, 4 * q : 4 * q + 4, :].bitcast(I32),
            )
        nc.sync.dma_start(out=w_raw[1][:], in_=w_rows[:, :, P : 2 * P])
        with nc.allow_non_contiguous_dma(reason="one value a partition"):
            nc.sync.dma_start(out=beta_sb[:], in_=beta.rearrange("(t p) o -> p (t o)", p=P))
        nc.sync.dma_start(src_sb[:], src)
        nc.sync.dma_start(out=field_sb[:], in_=field)
        nc.sync.dma_start(dst_sb[:], dst)
        with nc.allow_non_contiguous_dma(reason="one value a partition"):
            nc.sync.dma_start(out=lam_sb[:], in_=lam.rearrange("(t p) o -> p (t o)", p=P))

        lnc = keep.tile([P, D], F32, name="lnc")
        nc.scalar.activation(lnc[:], coup_v[:], ACT.Ln, bias=2.0**-64)
        ident = keep.tile([P, P], F32, name="ident")
        make_identity(nc, ident[:])

        xg = keep.tile([P, S], U32, name="xg", align_bytes=64)
        nc.vector.tensor_copy(xg[:], xw[:].bitcast(U32).indirect(offs_sb[:]))
        w_codes, w_scales = [], []
        w_bf = []
        for t in range(tiles):
            wb = keep.tile([P, P, 4], BF16, name="w_bf%d" % t, tag="w_bf%d" % t, align_bytes=64)
            nc.scalar.copy(out=wb[:], in_=w_raw[t][:].rearrange("p j m -> p m j"))
            w_bf.append(wb)
            w_codes.append(keep.tile([P, P], U32, name="w_codes%d" % t, align_bytes=64))
            w_scales.append(keep.tile([P, P], U8, name="w_scales%d" % t, align_bytes=64))

        def quantise(t):
            nc.vector.quantize_mx(
                out=w_codes[t][:].bitcast(FP8X4),
                scales=w_scales[t][:],
                in_=w_bf[t][:].rearrange("p m j -> p (m j)"),
            )

        def cols(h):
            return slice(h * HALF, (h + 1) * HALF)

        def lcols(h):
            return slice(h * HALF // 16, (h + 1) * HALF // 16)

        def groups(h):
            return slice(h * VH, (h + 1) * VH)

        def product(acc, t, c):
            nc.tensor.matmul_mx(
                out=acc,
                lhsT=w_codes[t][:].bitcast(FP8X4),
                lhsT_scale=w_scales[t][:],
                rhs=xg[:, c].bitcast(FP8X4),
                rhs_scale=sg[:, c],
                start=True,
                stop=True,
            )

        y = [keep.tile([P, S], F32, name="y%d" % t) for t in range(tiles)]
        early, late = slice(0, S - P), slice(S - P, S)

        def entries(c):
            return slice(c.start // 16, c.stop // 16)

        quantise(0)
        sg = keep.tile([P, S], U8, name="sg", tag="w_raw0", align_bytes=64)
        thirds = (slice(0, HALF), slice(HALF, S - P), late)
        for c in thirds:
            nc.vector.tensor_copy(sg[:, c], xs[:].indirect(offs_sb[:, entries(c)]))
        lnb = keep.tile([P, tiles], F32, name="lnb")
        nc.scalar.activation(lnb[:], beta_sb[:], ACT.Ln, bias=2.0**-64, scale=-1.0)
        root = keep.tile([P, tiles], F32, name="root", tag="w_raw1", align_bytes=64)
        root_lam = keep.tile([P, tiles], F32, name="root_lam")
        nc.scalar.activation(root[:], lnb[:], ACT.Exp, scale=0.5)
        for t in range(tiles):
            nc.scalar.activation(root_lam[:, t : t + 1], lam_sb[:, t : t + 1], ACT.Copy, scale=root[:, t : t + 1])
        accs = [bank(b, [P, c.stop - c.start], "acc%d" % b) for b, c in enumerate(thirds)]
        for acc, c in zip(accs, thirds):
            product(acc[:], 0, c)
        quantise(1)
        for acc, c in zip(accs, thirds):
            nc.vector.tensor_copy(out=y[0][:, c], in_=acc[:])
        acc_1 = bank(3, [P, S], "acc_1")
        product(acc_1[:], 1, slice(0, S))
        nc.scalar.copy(out=y[1][:], in_=acc_1[:])

        backs, tots = [], []
        for t in range(tiles):
            part = [
                keep.tile([P, HALF], F32, name="part%d_%d" % (t, h), tag="dg0" if (t, h) == (1, 1) else "part%d_%d" % (t, h))
                for h in range(2)
            ]
            dg = keep.tile([P, S], F32, name="dg%d" % t, tag="dg%d" % t)
            sq = keep.tile([P, D, V], F32, name="sq%d" % t, tag=("sq0", "chain")[t])
            nmu = keep.tile([P, V], F32, name="nmu%d" % t, tag=("chain", "nmu1")[t])
            sq_vd = sq[:].rearrange("p d v -> p v d")
            for h in range(2):
                nc.vector.tensor_tensor(
                    part[h][:], y[t][:].indirect(src_sb[:, lcols(h)]), field_sb[:, cols(h)], ALU.subtract
                )
            pieces = [cols(0), cols(1)] if t == 0 else [cols(0), slice(HALF, S - P), late]
            for c in pieces:
                g = slice(c.start // D, c.stop // D)
                nc.vector.tensor_tensor(dg[:, c], y[t][:].indirect(dst_sb[:, entries(c)]), part[c.start // HALF][:, c.start % HALF : c.start % HALF + c.stop - c.start], ALU.subtract)
                nc.scalar.activation(
                    sq_vd[:, g, :],
                    dg[:, c].rearrange("p (v d) -> p v d", d=D),
                    ACT.Square,
                    bias=root_lam[:, t : t + 1],
                    scale=root[:, t : t + 1],
                )
            for c in ([slice(0, S)] if t == 0 else [early, late]):
                g = slice(c.start // D, c.stop // D)
                nc.vector.tensor_reduce(nmu[:, g], sq_vd[:, g, :], AX.X, ALU.min, negate=True)
            turned = [bank((0, 1, 2, 6 + t)[d], [P, P], "turned%d_%d" % (t, d)) for d in range(D)]
            for d in range(D):
                nc.tensor.matmul(turned[d][:], sq[:, d, :], ident[:], start=True, stop=False, is_transpose=True)
            rate = keep.tile([P, D, P], F32, name="rate%d" % t)
            tot = bank(4 + t, [P, V], "tot%d" % t)
            for d in range(D):
                nc.tensor.matmul(turned[d][:], nmu[:], ident[:], start=False, stop=True, is_transpose=True)
            for d in range(D):
                nc.scalar.activation(rate[:, d, :], turned[d][:], ACT.Exp, bias=lnc[:, d : d + 1], scale=-1.0)
                nc.tensor.matmul(
                    tot[:], rate[:, d, :], ident[:], start=(d == 0), stop=(d == D - 1), is_transpose=True
                )
            back = bank(6 + t, [P, D, V], "back%d" % t)
            for d in range(D):
                nc.tensor.transpose(back[:, d, :], rate[:, d, :], ident[:])
            backs.append(back)
            tots.append(tot)

        for t in range(tiles):
            back, tot = backs[t], tots[t]
            inv = keep.tile([P, V], F32, name="inv%d" % t, tag=("dg1", "inv1")[t])
            res = keep.tile([P, S], F32, name="res%d" % t)
            for h in range(2):
                nc.vector.reciprocal(inv[:, groups(h)], tot[:, groups(h)])
            for h in range(2):
                nc.vector.tensor_tensor(
                    res[:, cols(h)].rearrange("p (v d) -> p v d", d=D),
                    back[:].rearrange("p d v -> p v d")[:, groups(h), :],
                    inv[:, groups(h)].unsqueeze(2).to_broadcast([P, VH, D]),
                    ALU.mult,
                )
                nc.sync.dma_start(out=out[t * P : (t + 1) * P, cols(h)], in_=res[:, cols(h)])
